import numpy as np
import ml_dtypes


def mxq(x, axis, fmt="e4m3"):
    dtype, down = {"e4m3": (ml_dtypes.float8_e4m3fn, 7), "e5m2": (ml_dtypes.float8_e5m2, 14)}[fmt]
    v = np.moveaxis(np.asarray(x, np.float32).astype(ml_dtypes.bfloat16).astype(np.float64), axis, -1)
    blocks = v.reshape(v.shape[:-1] + (-1, 32))
    amax = np.abs(blocks).max(-1, keepdims=True)
    byte = np.maximum(np.where(amax > 0, np.frexp(amax)[1] - 1 + 127, 0) - down, 1)
    scale = np.exp2(byte - 127.0)
    codes = (blocks / scale).astype(np.float32).astype(dtype).astype(np.float64)
    return np.moveaxis((codes * scale).reshape(v.shape), -1, axis)


WIDE = False


def mx_kscale(k):
    if not WIDE:
        return np.ones(k)
    levels = np.array([10, -10, 5, -5, 0])
    if k % 512:
        return np.exp2(np.random.permutation(np.resize(levels, k // 32))).repeat(32)
    a = np.empty((k // 512, 16))
    for p in range(k // 512):
        a[p, :8] = np.random.permutation(np.resize(levels, 8))
        for g in range(8):
            far = levels[np.abs(levels - a[p, g]) >= 10]
            a[p, g + 8] = far[np.random.randint(len(far))]
    return np.exp2(a.ravel()).repeat(32)


def f64(x):
    return np.asarray(x).astype(np.float64)


def striped(idx):
    return np.tile(idx.reshape(-1, 16).T, (8, 1)).astype(np.uint16)


def unstriped(offs):
    return offs[:16].T.reshape(-1).astype(np.int64)


E2M1 = np.array([0.0, 0.5, 1.0, 1.5, 2.0, 3.0, 4.0, 6.0, -0.0, -0.5, -1.0, -1.5, -2.0, -3.0, -4.0, -6.0])


def pack_weight(w, fmt):
    k, n = w.shape
    w = f64(np.asarray(w, np.float32).astype(ml_dtypes.bfloat16)).reshape(k // 32, 32, n)
    amax = np.abs(w).max(1)
    if fmt == "e4m3":
        byte = np.frexp(amax)[1] - 1 + 127 - 7
    else:
        mant, ex = np.frexp(amax / 6.0)
        byte = np.where(mant > 0.5, ex, ex - 1) + 127
    byte = np.clip(np.where(amax > 0, byte, 1), 1, 254)
    scaled = (w * np.exp2(127.0 - byte)[:, None, :]).reshape(k, n).astype(np.float32)
    by_word = np.ascontiguousarray(scaled.reshape(k // 512, 128, 4, n).transpose(0, 1, 3, 2))
    if fmt == "e4m3":
        words = by_word.astype(ml_dtypes.float8_e4m3fn).view(np.uint8)
    else:
        c = by_word.astype(ml_dtypes.float4_e2m1fn).view(np.uint8) & 0xF
        words = (c[..., 0::2] | (c[..., 1::2] << 4)).reshape(k // 512, 128, 2 * n)
    return np.ascontiguousarray(words), np.ascontiguousarray(byte.astype(np.uint8).reshape(k // 512, 16, n))


def unpack_weight(words, scales, fmt):
    g, _, n = scales.shape
    words = np.ascontiguousarray(words).reshape(g, 128, n, -1)
    if fmt == "e4m3":
        vals = words.view(ml_dtypes.float8_e4m3fn).astype(np.float64)
    else:
        nib = np.empty((g, 128, n, 4), np.uint8)
        nib[..., 0::2] = words & 0xF
        nib[..., 1::2] = words >> 4
        vals = E2M1[nib]
    vals = vals * np.repeat(np.exp2(scales.astype(np.float64) - 127.0), 8, axis=1)[..., None]
    return vals.transpose(0, 1, 3, 2).reshape(g * 512, n)


def gelu(v):
    return 0.5 * v * (1.0 + np.tanh(np.sqrt(2.0 / np.pi) * (v + 0.044715 * v**3)))


def bf(x):
    return np.asarray(x, np.float32).astype(ml_dtypes.bfloat16)


def planes(Y):
    n, m = Y.shape
    b = f64(bf(Y)).reshape(n // 32, 32, m)
    amax = np.abs(b).max(1)
    byte = np.clip(np.where(amax > 0, np.frexp(amax)[1] - 1 + 127 - 7, 1), 1, 254)
    codes = (b * np.exp2(127.0 - byte)[:, None, :]).reshape(n, m).astype(np.float32).astype(ml_dtypes.float8_e4m3fn).view(np.uint8)
    words = codes.reshape(n // 512, 128, 4, m).transpose(0, 1, 3, 2)
    return np.ascontiguousarray(words), np.ascontiguousarray(byte.astype(np.uint8).reshape(n // 512, 16, m))


K, T, S, H, P, N = 1536, 2048, 1024, 1024, 512, 512

def setup_inputs():
    n = np.random.standard_normal
    s = mx_kscale(K)[:, None]
    u = mx_kscale(H)[:, None]
    spread = np.exp(0.8 * n(N))[None, :]
    tab_words, tab_scales = pack_weight(n((K, T)) * s, "e4m3")
    w1 = n((K, H)) / np.sqrt(K) / s
    lamp = np.random.uniform(0.4, 1.2, (H, S))
    thr = n(H)
    tint = np.sign(n(H)) * np.random.uniform(2.5, 5.0, H) * u[:, 0]
    wear = n((H, P)) * u
    w2_words, w2_scales = pack_weight(2.4 * n((H, N)) / np.sqrt(H) / u * spread, "e2m1")
    w3 = n((H, N)) / np.sqrt(H) / u * spread
    return {"tab_words": tab_words, "tab_scales": tab_scales,
            "offs": striped(np.random.permutation(T)[:S]),
            "pos1": striped(np.random.permutation(S)[:P]),
            "pos2": striped(np.random.permutation(S)[:P]),
            "w1": w1.astype(np.float32), "lamp": lamp.astype(np.float32),
            "thr": thr.astype(np.float32), "tint": tint.astype(np.float32),
            "wear": wear.astype(np.float32),
            "w2_words": w2_words, "w2_scales": w2_scales,
            "w3": w3.astype(np.float32)}

def reference(tab_words, tab_scales, offs, pos1, pos2, w1, lamp, thr, tint, wear, w2_words, w2_scales, w3):
    v = unpack_weight(tab_words, tab_scales, "e4m3")[:, unstriped(offs)]
    h = (mxq(f64(w1), 0, "e4m3").T @ v) * f64(lamp)
    top = h.max(axis=1)
    a = 1.0 / (1.0 + np.exp(-(h[:, unstriped(pos1)] + f64(thr)[:, None])))
    c = np.exp(h[:, unstriped(pos2)] - top[:, None])
    f = mxq(a * c * f64(tint)[:, None], 0, "e4m3")
    d = mxq(a * f64(wear), 0, "e4m3")
    w2 = unpack_weight(w2_words, w2_scales, "e2m1")
    y = np.minimum(w2.T @ f, mxq(f64(w3), 0, "e4m3").T @ d)
    words, scales = planes(y)
    return y, words, scales

@@ -1,0 +1,290 @@
+from contextlib import ExitStack
+
+import concourse.mybir as mybir
+
+K, T, S, H, M, N = 1536, 2048, 1024, 1024, 512, 512
+FLOPS = 2 * K * H * S + 2 * 2 * H * N * M
+
+F32 = mybir.dt.float32
+BF16 = mybir.dt.bfloat16
+I32 = mybir.dt.int32
+U32 = mybir.dt.uint32
+U16 = mybir.dt.uint16
+U8 = mybir.dt.uint8
+FP8X4 = mybir.dt.float8_e4m3fn_x4
+FP4X4 = mybir.dt.float4_e2m1fn_x4
+ACT = mybir.ActivationFunctionType
+ALU = mybir.AluOpType
+AXIS = mybir.AxisListType
+
+P = 128
+PACK = 4
+G = P * PACK
+KP = K // G
+HP = H // G
+BANK = 512
+
+
+def tile_list_photochromic_fatigue_features_kernel(
+    tc, tab_words, tab_scales, offs, pos1, pos2, w1, lamp, thr, tint, wear, w2_words, w2_scales, w3,
+    out_0, out_1, out_2,
+):
+    nc = tc.nc
+    with ExitStack() as ctx:
+        keep = ctx.enter_context(tc.tile_pool(name="keep", bufs=1))
+        raw = ctx.enter_context(tc.tile_pool(name="raw", bufs=4))
+        rounded = ctx.enter_context(tc.tile_pool(name="rounded", bufs=4))
+        psum = ctx.enter_context(tc.psum_pool(name="psum", bufs=1))
+
+        def kept(shape, dtype, name):
+            return keep.tile(shape, dtype, name=name, align_bytes=64)
+
+        def bank(i):
+            return psum.tile([P, BANK], F32, name="bank%d" % i)
+
+        def load_rows(rows):
+            tile = raw.tile([P, PACK, G], F32, name="raw")
+            nc.sync.dma_start(out=tile[:], in_=rows.rearrange("(p j) c -> p j c", j=PACK))
+            return tile
+
+        def deal(src, scalar_share):
+            dst = rounded_tile()
+            dst_view = dst[:].rearrange("p (t q j) -> p q j t", t=PACK, j=PACK)
+            src_view = src[:].rearrange("p j (q t) -> p q j t", t=PACK)
+            if scalar_share > 0:
+                nc.scalar.copy(out=dst_view[:, :scalar_share], in_=src_view[:, :scalar_share])
+            if scalar_share < P:
+                nc.vector.tensor_copy(out=dst_view[:, scalar_share:], in_=src_view[:, scalar_share:])
+            return dst
+
+        def woven(ap):
+            return ap.rearrange("p (c i t) -> p c t i", i=4, t=PACK)
+
+        def planes4(ap):
+            return ap.rearrange("p t (c i) -> p c t i", i=4)
+
+        def quantise(src, name):
+            codes = kept([P, G], U32, name + "_codes")
+            scales = kept([P, G], U8, name + "_scales")
+            nc.vector.quantize_mx(out=codes[:].bitcast(FP8X4), scales=scales[:], in_=src[:])
+            return codes, scales
+
+        def rounded_tile():
+            return rounded.tile([P, PACK * G], BF16, name="rounded", align_bytes=64)
+
+        tab_sc = kept([P, T], U8, "tab_sc")
+        nc.gpsimd.memset(tab_sc[:].bitcast(I32), 0)
+        w2_sc_raw = kept([P, HP, N], U8, "w2_sc_raw")
+        nc.vector.memset(w2_sc_raw[:].rearrange("p a n -> p (a n)").bitcast(I32), 0)
+
+        offs_sb = keep.tile([P, S // 16], U16, name="offs_sb")
+        nc.sync.dma_start(offs_sb[:], offs)
+        pos1_sb = keep.tile([P, M // 16], U16, name="pos1_sb")
+        nc.sync.dma_start(pos1_sb[:], pos1)
+        pos2_sb = keep.tile([P, M // 16], U16, name="pos2_sb")
+        nc.sync.dma_start(pos2_sb[:], pos2)
+        thr_sb = keep.tile([P, HP, PACK], F32, name="bias")
+        nc.sync.dma_start(out=thr_sb[:], in_=thr.rearrange("(b p t) -> p b t", p=P, t=PACK))
+        tint_sb = keep.tile([P, HP, PACK], F32, name="tint_sb")
+        nc.sync.dma_start(out=tint_sb[:], in_=tint.rearrange("(b p t) -> p b t", p=P, t=PACK))
+        w2_raw = kept([P, HP, 2 * N], U8, "w2_raw")
+        nc.sync.dma_start(out=w2_raw[:].bitcast(I32), in_=w2_words.rearrange("a p n -> p a n").bitcast(I32))
+        tab = []
+        w1_raw = {}
+        for a in range(KP):
+            w1_raw[0, a] = load_rows(w1[a * G : (a + 1) * G, 0:G])
+            words = kept([P, T], U32, "tab%d" % a)
+            nc.sync.dma_start(
+                out=words[:].bitcast(I32), in_=tab_words[a].rearrange("p n i -> p (n i)").bitcast(I32)
+            )
+            tab.append(words)
+            if a == 0:
+                for q in range(4):
+                    nc.scalar.dma_start(
+                        out=tab_sc[32 * q : 32 * q + 4 * KP, :].bitcast(I32),
+                        in_=tab_scales[:, 4 * q : 4 * q + 4, :].bitcast(I32),
+                    )
+        for q in range(4):
+            nc.sync.dma_start(
+                out=w2_sc_raw[32 * q : 32 * q + 4].bitcast(I32),
+                in_=w2_scales[:, 4 * q : 4 * q + 4, :].rearrange("a r n -> r a n").bitcast(I32),
+            )
+
+        h = {}
+
+        def load_lamp(b):
+            rows = lamp[b * G : (b + 1) * G, :].rearrange("(p t) s -> p t s", t=PACK)
+            for t in range(PACK):
+                h[b, t] = kept([P, S], F32, "h%d%d" % (b, t))
+                nc.sync.dma_start(out=h[b, t][:], in_=rows[:, t, :])
+
+        load_lamp(0)
+
+        w2_dealt = kept([P, HP, 2 * N], U8, "w2_dealt")
+        nc.vector.tensor_copy(
+            out=w2_dealt[:].rearrange("p a (t q e) -> p a q t e", t=PACK, e=2),
+            in_=w2_raw[:].rearrange("p a (q t e) -> p a q t e", t=PACK, e=2),
+        )
+
+        picked = []
+        picked_sc = kept([P, S], U8, "picked_sc")
+        nc.vector.tensor_copy(out=picked_sc[:], in_=tab_sc[:].indirect(offs_sb[:]))
+
+        def first_pass(acc, a, codes, scales):
+            for t in range(PACK):
+                for half in range(2):
+                    cols = slice(half * BANK, (half + 1) * BANK)
+                    nc.tensor.matmul_mx(
+                        out=acc[t, half][:],
+                        lhsT=codes[:, t * P : (t + 1) * P].bitcast(FP8X4),
+                        lhsT_scale=scales[:, t * P : (t + 1) * P],
+                        rhs=picked[a][half][:].bitcast(FP8X4),
+                        rhs_scale=picked_sc[4 * a : P, cols],
+                        start=(a == 0),
+                        stop=(a == KP - 1),
+                    )
+
+        gate = {}
+        tinted = {}
+
+        def scores(acc, b):
+            gate[b] = kept([P, PACK, M], F32, "gate%d" % b)
+
+            for t in range(PACK):
+                for half in range(2):
+                    cols = slice(half * BANK, (half + 1) * BANK)
+                    nc.vector.tensor_tensor(
+                        out=h[b, t][:, cols], in0=acc[t, half][:], in1=h[b, t][:, cols], op=ALU.mult
+                    )
+                nc.scalar.activation(
+                    out=gate[b][:, t, :], in_=h[b, t][:].indirect(pos1_sb[:]), func=ACT.Sigmoid,
+                    bias=thr_sb[:, b, t : t + 1],
+                )
+
+
+        acc = {(t, half): bank(2 * t + half) for t in range(PACK) for half in range(2)}
+        for a in range(KP):
+            dealt = deal(w1_raw[0, a], 64 if a == KP - 1 else P)
+            codes, scales = quantise(dealt, "w1_0%d" % a)
+            halves = []
+            for half in range(2):
+                words = kept([P, BANK], U32, "picked%d%d" % (a, half))
+                nc.vector.tensor_copy(
+                    out=words[:], in_=tab[a][:].indirect(offs_sb[:, half * BANK // 16 : (half + 1) * BANK // 16])
+                )
+                halves.append(words)
+            picked.append(halves)
+            first_pass(acc, a, codes, scales)
+
+        w2_sc = kept([P, HP, N], U8, "w2_sc")
+        nc.vector.tensor_copy(
+            out=w2_sc[:].rearrange("p a (t q) -> p a q t", t=PACK),
+            in_=w2_sc_raw[:].rearrange("p a (q t) -> p a q t", t=PACK),
+        )
+
+        for a in range(KP):
+            w1_raw[1, a] = load_rows(w1[a * G : (a + 1) * G, G : 2 * G])
+        w3_raw = {0: load_rows(w3[0:G, :])}
+        load_lamp(1)
+        wear_sb = {}
+        for b in range(HP):
+            wear_sb[b] = kept([P, PACK, M], F32, "wear%d" % b)
+            nc.sync.dma_start(
+                out=wear_sb[b][:], in_=wear[b * G : (b + 1) * G, :].rearrange("(p t) m -> p t m", t=PACK)
+            )
+        w3_raw[1] = load_rows(w3[G : 2 * G, :])
+
+        scores(acc, 0)
+        acc = {(t, half): bank(2 * t + half) for t in range(PACK) for half in range(2)}
+        for a in range(KP):
+            dealt = deal(w1_raw[1, a], 0 if a == KP - 1 else P)
+            codes, scales = quantise(dealt, "w1_1%d" % a)
+            first_pass(acc, a, codes, scales)
+        w3_dealt = {0: deal(w3_raw[0], P)}
+        scores(acc, 1)
+
+        top = keep.tile([P, HP, PACK], F32, name="top")
+        neg_top = keep.tile([P, HP, PACK], F32, name="bias")
+        for b in range(HP):
+            for t in range(PACK):
+                nc.vector.reduce_max(out=top[:, b, t : t + 1], in_=h[b, t][:], axis=AXIS.X)
+            nc.vector.tensor_scalar(
+                out=neg_top[:, b, :], in0=top[:, b, :], scalar1=-1.0, scalar2=None, op0=ALU.mult
+            )
+
+        def second_pass(acc2, b, lhs, lhs_scale, codes, scales):
+            for t in range(PACK):
+                nc.tensor.matmul_mx(
+                    out=acc2[t][:], lhsT=lhs(t), lhsT_scale=lhs_scale[:, t * P : (t + 1) * P],
+                    rhs=codes[:].bitcast(FP8X4), rhs_scale=scales[:],
+                    start=(b == 0), stop=(b == HP - 1),
+                )
+
+        worn_acc = [bank(t) for t in range(PACK)]
+        joint_acc = [bank(PACK + t) for t in range(PACK)]
+
+        def worn_product(b):
+            d = rounded_tile()
+            nc.vector.tensor_tensor(
+                out=woven(d[:]), in0=planes4(gate[b][:]), in1=planes4(wear_sb[b][:]), op=ALU.mult
+            )
+            return d
+
+        def worn_product_g(b):
+            d = rounded_tile()
+            nc.gpsimd.tensor_tensor(
+                out=woven(d[:]), in0=planes4(gate[b][:]), in1=planes4(wear_sb[b][:]), op=ALU.mult
+            )
+            return d
+
+        def worn(b, d):
+            d_codes, d_scales = quantise(d, "d%d" % b)
+            w3_codes, w3_scales = quantise(w3_dealt[b], "w3_%d" % b)
+            second_pass(
+                worn_acc, b, lambda t: w3_codes[:, t * P : (t + 1) * P].bitcast(FP8X4), w3_scales, d_codes, d_scales
+            )
+
+        def joint(b, weave):
+            c = kept([P, PACK, M], F32, "c%d" % b)
+            for t in range(PACK):
+                nc.scalar.activation(
+                    out=c[:, t, :], in_=h[b, t][:].indirect(pos2_sb[:]), func=ACT.Exp,
+                    bias=neg_top[:, b, t : t + 1],
+                )
+                nc.vector.scalar_tensor_tensor(
+                    out=c[:, t, :], in0=gate[b][:, t, :], scalar=tint_sb[:, b, t : t + 1], in1=c[:, t, :],
+                    op0=ALU.mult, op1=ALU.mult,
+                )
+            f = rounded_tile()
+            weave(out=woven(f[:]), in_=planes4(c[:]))
+            f_codes, f_scales = quantise(f, "f%d" % b)
+            second_pass(
+                joint_acc, b, lambda t: w2_dealt[:, b, 2 * t * P : 2 * (t + 1) * P].bitcast(FP4X4),
+                w2_sc[:, b, :], f_codes, f_scales,
+            )
+
+        worn(0, worn_product(0))
+        d1 = worn_product(1)
+        joint(0, nc.scalar.copy)
+        w3_dealt[1] = deal(w3_raw[1], 128)
+        worn(1, d1)
+        joint(1, nc.vector.tensor_copy)
+
+        y = kept([P, PACK, M], F32, "y")
+        y_rows = out_0.rearrange("(p t) m -> p t m", t=PACK)
+        for t in range(PACK):
+            nc.scalar.copy(out=y[:, t, :], in_=worn_acc[t][:])
+        for t in range(PACK):
+            nc.vector.tensor_tensor(out=y[:, t, :], in0=joint_acc[t][:], in1=y[:, t, :], op=ALU.min)
+            nc.sync.dma_start(out=y_rows[:, t, :], in_=y[:, t, :])
+        y_rounded = rounded_tile()
+        nc.vector.tensor_copy(out=woven(y_rounded[:]), in_=planes4(y[:]))
+        y_codes, y_scales = quantise(y_rounded, "y")
+        nc.sync.dma_start(
+            out=out_1[0].rearrange("p m i -> p (m i)").bitcast(I32), in_=y_codes[:].bitcast(I32)
+        )
+        for q in range(4):
+            queue = nc.scalar if q % 2 == 0 else nc.sync
+            queue.dma_start(
+                out=out_2[0, 4 * q : 4 * q + 4, :].bitcast(I32), in_=y_scales[32 * q : 32 * q + 4, :].bitcast(I32)
+            )

@@ -19,10 +19,17 @@ AXIS = mybir.AxisListType
 
 P = 128
 PACK = 4
-G = P * PACK
-KP = K // G
-HP = H // G
+GROUP = P * PACK
+K_GROUPS = K // GROUP
+H_GROUPS = H // GROUP
 BANK = 512
+S_BANKS = S // BANK
+QUADS = 4
+LINE = 4
+PER_COLUMN = 16
+
+WEAVE_SHARE = 40
+FIRST_WEIGHT_SHARE = 64
 
 
 def tile_list_photochromic_fatigue_features_kernel(
@@ -32,7 +39,7 @@ def tile_list_photochromic_fatigue_features_kernel(
     nc = tc.nc
     with ExitStack() as ctx:
         keep = ctx.enter_context(tc.tile_pool(name="keep", bufs=1))
-        raw = ctx.enter_context(tc.tile_pool(name="raw", bufs=4))
+        raw = ctx.enter_context(tc.tile_pool(name="raw", bufs=7))
         rounded = ctx.enter_context(tc.tile_pool(name="rounded", bufs=4))
         psum = ctx.enter_context(tc.psum_pool(name="psum", bufs=1))
 
@@ -42,249 +49,254 @@ def tile_list_photochromic_fatigue_features_kernel(
         def bank(i):
             return psum.tile([P, BANK], F32, name="bank%d" % i)
 
-        def load_rows(rows):
-            tile = raw.tile([P, PACK, G], F32, name="raw")
-            nc.sync.dma_start(out=tile[:], in_=rows.rearrange("(p j) c -> p j c", j=PACK))
+        def rounded_tile():
+            return rounded.tile([P, PACK * GROUP], BF16, name="rounded", align_bytes=64)
+
+        def shared_copy(dst, src, scalar_share):
+            if scalar_share > 0:
+                nc.scalar.copy(out=dst[:, :scalar_share], in_=src[:, :scalar_share])
+            if scalar_share < P:
+                nc.vector.tensor_copy(out=dst[:, scalar_share:], in_=src[:, scalar_share:])
+
+        def load_weight(rows):
+            tile = raw.tile([P, PACK, GROUP], F32, name="raw")
+            nc.sync.dma_start(out=tile[:], in_=rows.rearrange("(p i) c -> p i c", i=PACK))
             return tile
 
         def deal(src, scalar_share):
             dst = rounded_tile()
-            dst_view = dst[:].rearrange("p (t q j) -> p q j t", t=PACK, j=PACK)
-            src_view = src[:].rearrange("p j (q t) -> p q j t", t=PACK)
-            if scalar_share > 0:
-                nc.scalar.copy(out=dst_view[:, :scalar_share], in_=src_view[:, :scalar_share])
-            if scalar_share < P:
-                nc.vector.tensor_copy(out=dst_view[:, scalar_share:], in_=src_view[:, scalar_share:])
+            shared_copy(
+                dst[:].rearrange("p (t q i) -> p q i t", t=PACK, i=PACK),
+                src[:].rearrange("p i (q t) -> p q i t", t=PACK),
+                scalar_share,
+            )
             return dst
 
-        def woven(ap):
-            return ap.rearrange("p (c i t) -> p c t i", i=4, t=PACK)
+        def woven(tile):
+            return tile[:].rearrange("p (c e t) -> p c t e", e=LINE, t=PACK)
 
-        def planes4(ap):
-            return ap.rearrange("p t (c i) -> p c t i", i=4)
+        def by_lines(tile):
+            return tile[:].rearrange("p t (c e) -> p c t e", e=LINE)
+
+        def weave(src, scalar_share):
+            dst = rounded_tile()
+            shared_copy(woven(dst), by_lines(src), scalar_share)
+            return dst
 
         def quantise(src, name):
-            codes = kept([P, G], U32, name + "_codes")
-            scales = kept([P, G], U8, name + "_scales")
+            codes = kept([P, GROUP], U32, name + "_codes")
+            scales = kept([P, GROUP], U8, name + "_scales")
             nc.vector.quantize_mx(out=codes[:].bitcast(FP8X4), scales=scales[:], in_=src[:])
             return codes, scales
 
-        def rounded_tile():
-            return rounded.tile([P, PACK * G], BF16, name="rounded", align_bytes=64)
+        def load_list(src, entries, name):
+            tile = keep.tile([P, entries // PER_COLUMN], U16, name=name)
+            nc.sync.dma_start(tile[:], src)
+            return tile
 
-        tab_sc = kept([P, T], U8, "tab_sc")
-        nc.gpsimd.memset(tab_sc[:].bitcast(I32), 0)
-        w2_sc_raw = kept([P, HP, N], U8, "w2_sc_raw")
-        nc.vector.memset(w2_sc_raw[:].rearrange("p a n -> p (a n)").bitcast(I32), 0)
+        def load_row_values(src, name):
+            tile = keep.tile([P, H_GROUPS, PACK], F32, name=name)
+            nc.sync.dma_start(out=tile[:], in_=src.rearrange("(b p t) -> p b t", p=P, t=PACK))
+            return tile
 
-        offs_sb = keep.tile([P, S // 16], U16, name="offs_sb")
-        nc.sync.dma_start(offs_sb[:], offs)
-        pos1_sb = keep.tile([P, M // 16], U16, name="pos1_sb")
-        nc.sync.dma_start(pos1_sb[:], pos1)
-        pos2_sb = keep.tile([P, M // 16], U16, name="pos2_sb")
-        nc.sync.dma_start(pos2_sb[:], pos2)
-        thr_sb = keep.tile([P, HP, PACK], F32, name="bias")
-        nc.sync.dma_start(out=thr_sb[:], in_=thr.rearrange("(b p t) -> p b t", p=P, t=PACK))
-        tint_sb = keep.tile([P, HP, PACK], F32, name="tint_sb")
-        nc.sync.dma_start(out=tint_sb[:], in_=tint.rearrange("(b p t) -> p b t", p=P, t=PACK))
-        w2_raw = kept([P, HP, 2 * N], U8, "w2_raw")
-        nc.sync.dma_start(out=w2_raw[:].bitcast(I32), in_=w2_words.rearrange("a p n -> p a n").bitcast(I32))
-        tab = []
-        w1_raw = {}
-        for a in range(KP):
-            w1_raw[0, a] = load_rows(w1[a * G : (a + 1) * G, 0:G])
-            words = kept([P, T], U32, "tab%d" % a)
+        table, w1_raw, h, wear_sb = {}, {}, {}, {}
+
+        def load_table(a):
+            table[a] = kept([P, T], U32, "table%d" % a)
             nc.sync.dma_start(
-                out=words[:].bitcast(I32), in_=tab_words[a].rearrange("p n i -> p (n i)").bitcast(I32)
-            )
-            tab.append(words)
-            if a == 0:
-                for q in range(4):
-                    nc.scalar.dma_start(
-                        out=tab_sc[32 * q : 32 * q + 4 * KP, :].bitcast(I32),
-                        in_=tab_scales[:, 4 * q : 4 * q + 4, :].bitcast(I32),
-                    )
-        for q in range(4):
-            nc.sync.dma_start(
-                out=w2_sc_raw[32 * q : 32 * q + 4].bitcast(I32),
-                in_=w2_scales[:, 4 * q : 4 * q + 4, :].rearrange("a r n -> r a n").bitcast(I32),
+                out=table[a][:].bitcast(I32), in_=tab_words[a].rearrange("p n i -> p (n i)").bitcast(I32)
             )
 
-        h = {}
+        def load_w1(b, a):
+            w1_raw[b, a] = load_weight(w1[a * GROUP : (a + 1) * GROUP, b * GROUP : (b + 1) * GROUP])
 
-        def load_lamp(b):
-            rows = lamp[b * G : (b + 1) * G, :].rearrange("(p t) s -> p t s", t=PACK)
-            for t in range(PACK):
-                h[b, t] = kept([P, S], F32, "h%d%d" % (b, t))
-                nc.sync.dma_start(out=h[b, t][:], in_=rows[:, t, :])
+        def load_lamp(b, t):
+            h[b, t] = kept([P, S], F32, "h%d%d" % (b, t))
+            rows = lamp[b * GROUP : (b + 1) * GROUP, :].rearrange("(p t) s -> p t s", t=PACK)
+            nc.sync.dma_start(out=h[b, t][:], in_=rows[:, t, :])
 
-        load_lamp(0)
-
-        w2_dealt = kept([P, HP, 2 * N], U8, "w2_dealt")
-        nc.vector.tensor_copy(
-            out=w2_dealt[:].rearrange("p a (t q e) -> p a q t e", t=PACK, e=2),
-            in_=w2_raw[:].rearrange("p a (q t e) -> p a q t e", t=PACK, e=2),
-        )
-
-        picked = []
-        picked_sc = kept([P, S], U8, "picked_sc")
-        nc.vector.tensor_copy(out=picked_sc[:], in_=tab_sc[:].indirect(offs_sb[:]))
-
-        def first_pass(acc, a, codes, scales):
-            for t in range(PACK):
-                for half in range(2):
-                    cols = slice(half * BANK, (half + 1) * BANK)
-                    nc.tensor.matmul_mx(
-                        out=acc[t, half][:],
-                        lhsT=codes[:, t * P : (t + 1) * P].bitcast(FP8X4),
-                        lhsT_scale=scales[:, t * P : (t + 1) * P],
-                        rhs=picked[a][half][:].bitcast(FP8X4),
-                        rhs_scale=picked_sc[4 * a : P, cols],
-                        start=(a == 0),
-                        stop=(a == KP - 1),
-                    )
-
-        gate = {}
-        tinted = {}
-
-        def scores(acc, b):
-            gate[b] = kept([P, PACK, M], F32, "gate%d" % b)
-
-            for t in range(PACK):
-                for half in range(2):
-                    cols = slice(half * BANK, (half + 1) * BANK)
-                    nc.vector.tensor_tensor(
-                        out=h[b, t][:, cols], in0=acc[t, half][:], in1=h[b, t][:, cols], op=ALU.mult
-                    )
-                nc.scalar.activation(
-                    out=gate[b][:, t, :], in_=h[b, t][:].indirect(pos1_sb[:]), func=ACT.Sigmoid,
-                    bias=thr_sb[:, b, t : t + 1],
-                )
-
-
-        acc = {(t, half): bank(2 * t + half) for t in range(PACK) for half in range(2)}
-        for a in range(KP):
-            dealt = deal(w1_raw[0, a], 64 if a == KP - 1 else P)
-            codes, scales = quantise(dealt, "w1_0%d" % a)
-            halves = []
-            for half in range(2):
-                words = kept([P, BANK], U32, "picked%d%d" % (a, half))
-                nc.vector.tensor_copy(
-                    out=words[:], in_=tab[a][:].indirect(offs_sb[:, half * BANK // 16 : (half + 1) * BANK // 16])
-                )
-                halves.append(words)
-            picked.append(halves)
-            first_pass(acc, a, codes, scales)
-
-        w2_sc = kept([P, HP, N], U8, "w2_sc")
-        nc.vector.tensor_copy(
-            out=w2_sc[:].rearrange("p a (t q) -> p a q t", t=PACK),
-            in_=w2_sc_raw[:].rearrange("p a (q t) -> p a q t", t=PACK),
-        )
-
-        for a in range(KP):
-            w1_raw[1, a] = load_rows(w1[a * G : (a + 1) * G, G : 2 * G])
-        w3_raw = {0: load_rows(w3[0:G, :])}
-        load_lamp(1)
-        wear_sb = {}
-        for b in range(HP):
+        def load_wear(b):
             wear_sb[b] = kept([P, PACK, M], F32, "wear%d" % b)
+            rows = wear[b * GROUP : (b + 1) * GROUP, :].rearrange("(p t) m -> p t m", t=PACK)
+            nc.sync.dma_start(out=wear_sb[b][:], in_=rows)
+
+        table_scales = kept([P, T], U8, "table_scales")
+        nc.vector.memset(table_scales[:].bitcast(I32), 0)
+        w2_scales_raw = kept([P, H_GROUPS, N], U8, "w2_scales_raw")
+        nc.gpsimd.memset(w2_scales_raw[:].rearrange("p b n -> p (b n)").bitcast(I32), 0)
+
+        offs_sb = load_list(offs, S, "offs_sb")
+        w2_raw = kept([P, H_GROUPS, 2 * N], U8, "w2_raw")
+        nc.sync.dma_start(out=w2_raw[:].bitcast(I32), in_=w2_words.rearrange("b p n -> p b n").bitcast(I32))
+        load_table(0)
+        load_w1(0, 0)
+        for quad in range(QUADS):
             nc.sync.dma_start(
-                out=wear_sb[b][:], in_=wear[b * G : (b + 1) * G, :].rearrange("(p t) m -> p t m", t=PACK)
+                out=table_scales[32 * quad : 32 * quad + 4 * K_GROUPS, :].bitcast(I32),
+                in_=tab_scales[:, 4 * quad : 4 * quad + 4, :].bitcast(I32),
             )
-        w3_raw[1] = load_rows(w3[G : 2 * G, :])
+        load_table(1)
+        load_w1(0, 1)
+        for quad in range(QUADS):
+            nc.sync.dma_start(
+                out=w2_scales_raw[32 * quad : 32 * quad + 4].bitcast(I32),
+                in_=w2_scales[:, 4 * quad : 4 * quad + 4, :].rearrange("b r n -> r b n").bitcast(I32),
+            )
+        load_table(2)
+        load_w1(0, 2)
+        pos1_sb = load_list(pos1, M, "pos1_sb")
+        thr_sb = load_row_values(thr, "look_bias")
+        load_lamp(0, 0)
+        load_w1(1, 0)
+        load_lamp(0, 1)
+        load_w1(1, 1)
+        load_lamp(0, 2)
+        load_lamp(0, 3)
+        load_w1(1, 2)
+        tint_sb = load_row_values(tint, "tint_sb")
+        pos2_sb = load_list(pos2, M, "pos2_sb")
+        w3_raw = {0: load_weight(w3[:GROUP, :])}
+        for t in range(PACK):
+            load_lamp(1, t)
+        for b in range(H_GROUPS):
+            load_wear(b)
+        w3_raw[1] = load_weight(w3[GROUP:, :])
 
-        scores(acc, 0)
-        acc = {(t, half): bank(2 * t + half) for t in range(PACK) for half in range(2)}
-        for a in range(KP):
-            dealt = deal(w1_raw[1, a], 0 if a == KP - 1 else P)
-            codes, scales = quantise(dealt, "w1_1%d" % a)
-            first_pass(acc, a, codes, scales)
+        w2_dealt = kept([P, H_GROUPS, 2 * N], U8, "w2_dealt")
+        nc.vector.tensor_copy(
+            out=w2_dealt[:].rearrange("p b (t q e) -> p b q t e", t=PACK, e=2),
+            in_=w2_raw[:].rearrange("p b (q t e) -> p b q t e", t=PACK, e=2),
+        )
+
+        picked = {}
+        picked_scales = kept([P, S], U8, "picked_scales")
+
+        def first_product(acc, a, weight, t):
+            codes, scales = weight
+            for half in range(S_BANKS):
+                nc.tensor.matmul_mx(
+                    out=acc[t, half][:],
+                    lhsT=codes[:, t * P : (t + 1) * P].bitcast(FP8X4),
+                    lhsT_scale=scales[:, t * P : (t + 1) * P],
+                    rhs=picked[a, half][:].bitcast(FP8X4),
+                    rhs_scale=picked_scales[4 * a : P, half * BANK : (half + 1) * BANK],
+                    start=(a == 0),
+                    stop=(a == K_GROUPS - 1),
+                )
+
+        def first_banks():
+            return {(t, half): bank(S_BANKS * t + half) for t in range(PACK) for half in range(S_BANKS)}
+
+        def score(acc, b, t):
+            for half in range(S_BANKS):
+                part = h[b, t][:, half * BANK : (half + 1) * BANK]
+                nc.vector.tensor_tensor(out=part, in0=acc[t, half][:], in1=part, op=ALU.mult)
+
+        gate = {b: kept([P, PACK, M], F32, "gate%d" % b) for b in range(H_GROUPS)}
+
+        def look_gate(b, t):
+            nc.scalar.activation(
+                out=gate[b][:, t, :], in_=h[b, t][:].indirect(pos1_sb[:]), func=ACT.Sigmoid,
+                bias=thr_sb[:, b, t : t + 1],
+            )
+
+        acc = first_banks()
+        for a in range(K_GROUPS):
+            weight = quantise(deal(w1_raw[0, a], FIRST_WEIGHT_SHARE if a == K_GROUPS - 1 else P), "w1_0%d" % a)
+            for half in range(S_BANKS):
+                picked[a, half] = kept([P, BANK], U32, "picked%d%d" % (a, half))
+                entries = offs_sb[:, half * BANK // PER_COLUMN : (half + 1) * BANK // PER_COLUMN]
+                nc.vector.tensor_copy(out=picked[a, half][:], in_=table[a][:].indirect(entries))
+            if a == 0:
+                nc.vector.tensor_copy(out=picked_scales[:], in_=table_scales[:].indirect(offs_sb[:]))
+            for t in range(PACK):
+                first_product(acc, a, weight, t)
+
+        for t in range(PACK):
+            score(acc, 0, t)
+        acc = first_banks()
+        weights = [quantise(deal(w1_raw[1, a], 0 if a == K_GROUPS - 1 else P), "w1_1%d" % a) for a in range(K_GROUPS)]
+        for t in range(PACK):
+            first_product(acc, 0, weights[0], t)
+        for t in range(PACK):
+            for a in range(1, K_GROUPS):
+                first_product(acc, a, weights[a], t)
+        for t in range(PACK):
+            look_gate(0, t)
         w3_dealt = {0: deal(w3_raw[0], P)}
-        scores(acc, 1)
+        for t in range(PACK):
+            score(acc, 1, t)
+            look_gate(1, t)
 
-        top = keep.tile([P, HP, PACK], F32, name="top")
-        neg_top = keep.tile([P, HP, PACK], F32, name="bias")
-        for b in range(HP):
+        w2_scales_dealt = kept([P, H_GROUPS, N], U8, "w2_scales_dealt")
+        nc.vector.tensor_copy(
+            out=w2_scales_dealt[:].rearrange("p b (t q) -> p b q t", t=PACK),
+            in_=w2_scales_raw[:].rearrange("p b (q t) -> p b q t", t=PACK),
+        )
+
+        top = keep.tile([P, H_GROUPS, PACK], F32, name="top")
+        neg_top = keep.tile([P, H_GROUPS, PACK], F32, name="look_bias")
+        for b in range(H_GROUPS):
             for t in range(PACK):
                 nc.vector.reduce_max(out=top[:, b, t : t + 1], in_=h[b, t][:], axis=AXIS.X)
-            nc.vector.tensor_scalar(
-                out=neg_top[:, b, :], in0=top[:, b, :], scalar1=-1.0, scalar2=None, op0=ALU.mult
-            )
-
-        def second_pass(acc2, b, lhs, lhs_scale, codes, scales):
-            for t in range(PACK):
-                nc.tensor.matmul_mx(
-                    out=acc2[t][:], lhsT=lhs(t), lhsT_scale=lhs_scale[:, t * P : (t + 1) * P],
-                    rhs=codes[:].bitcast(FP8X4), rhs_scale=scales[:],
-                    start=(b == 0), stop=(b == HP - 1),
-                )
+            nc.vector.tensor_scalar(out=neg_top[:, b, :], in0=top[:, b, :], scalar1=-1.0, scalar2=None, op0=ALU.mult)
 
         worn_acc = [bank(t) for t in range(PACK)]
         joint_acc = [bank(PACK + t) for t in range(PACK)]
 
-        def worn_product(b):
-            d = rounded_tile()
-            nc.vector.tensor_tensor(
-                out=woven(d[:]), in0=planes4(gate[b][:]), in1=planes4(wear_sb[b][:]), op=ALU.mult
+        def second_product(out, b, lhs, lhs_scale, moving):
+            codes, scales = moving
+            nc.tensor.matmul_mx(
+                out=out[:], lhsT=lhs, lhsT_scale=lhs_scale, rhs=codes[:].bitcast(FP8X4), rhs_scale=scales[:],
+                start=(b == 0), stop=(b == H_GROUPS - 1),
             )
+
+        def worn_values(b, engine):
+            d = rounded_tile()
+            engine.tensor_tensor(out=woven(d), in0=by_lines(gate[b]), in1=by_lines(wear_sb[b]), op=ALU.mult)
             return d
 
-        def worn_product_g(b):
-            d = rounded_tile()
-            nc.gpsimd.tensor_tensor(
-                out=woven(d[:]), in0=planes4(gate[b][:]), in1=planes4(wear_sb[b][:]), op=ALU.mult
-            )
-            return d
+        def worn_product(b, d):
+            moving = quantise(d, "d%d" % b)
+            codes, scales = quantise(w3_dealt[b], "w3_%d" % b)
+            for t in range(PACK):
+                cols = slice(t * P, (t + 1) * P)
+                second_product(worn_acc[t], b, codes[:, cols].bitcast(FP8X4), scales[:, cols], moving)
 
-        def worn(b, d):
-            d_codes, d_scales = quantise(d, "d%d" % b)
-            w3_codes, w3_scales = quantise(w3_dealt[b], "w3_%d" % b)
-            second_pass(
-                worn_acc, b, lambda t: w3_codes[:, t * P : (t + 1) * P].bitcast(FP8X4), w3_scales, d_codes, d_scales
-            )
-
-        def joint(b, weave):
+        def joint_product(b, scalar_share):
             c = kept([P, PACK, M], F32, "c%d" % b)
             for t in range(PACK):
                 nc.scalar.activation(
-                    out=c[:, t, :], in_=h[b, t][:].indirect(pos2_sb[:]), func=ACT.Exp,
-                    bias=neg_top[:, b, t : t + 1],
+                    out=c[:, t, :], in_=h[b, t][:].indirect(pos2_sb[:]), func=ACT.Exp, bias=neg_top[:, b, t : t + 1]
                 )
                 nc.vector.scalar_tensor_tensor(
                     out=c[:, t, :], in0=gate[b][:, t, :], scalar=tint_sb[:, b, t : t + 1], in1=c[:, t, :],
                     op0=ALU.mult, op1=ALU.mult,
                 )
-            f = rounded_tile()
-            weave(out=woven(f[:]), in_=planes4(c[:]))
-            f_codes, f_scales = quantise(f, "f%d" % b)
-            second_pass(
-                joint_acc, b, lambda t: w2_dealt[:, b, 2 * t * P : 2 * (t + 1) * P].bitcast(FP4X4),
-                w2_sc[:, b, :], f_codes, f_scales,
-            )
+            moving = quantise(weave(c, scalar_share), "f%d" % b)
+            for t in range(PACK):
+                lhs = w2_dealt[:, b, 2 * t * P : 2 * (t + 1) * P].bitcast(FP4X4)
+                second_product(joint_acc[t], b, lhs, w2_scales_dealt[:, b, t * P : (t + 1) * P], moving)
 
-        worn(0, worn_product(0))
-        d1 = worn_product(1)
-        joint(0, nc.scalar.copy)
-        w3_dealt[1] = deal(w3_raw[1], 128)
-        worn(1, d1)
-        joint(1, nc.vector.tensor_copy)
+        worn_product(0, worn_values(0, nc.vector))
+        d_last = worn_values(1, nc.vector)
+        joint_product(0, 0)
+        joint_product(1, WEAVE_SHARE)
+        w3_dealt[1] = deal(w3_raw[1], P)
+        worn_product(1, d_last)
 
-        y = kept([P, PACK, M], F32, "y")
+        y = kept([P, PACK, M], F32, "c0")
         y_rows = out_0.rearrange("(p t) m -> p t m", t=PACK)
         for t in range(PACK):
             nc.scalar.copy(out=y[:, t, :], in_=worn_acc[t][:])
         for t in range(PACK):
             nc.vector.tensor_tensor(out=y[:, t, :], in0=joint_acc[t][:], in1=y[:, t, :], op=ALU.min)
             nc.sync.dma_start(out=y_rows[:, t, :], in_=y[:, t, :])
-        y_rounded = rounded_tile()
-        nc.vector.tensor_copy(out=woven(y_rounded[:]), in_=planes4(y[:]))
-        y_codes, y_scales = quantise(y_rounded, "y")
-        nc.sync.dma_start(
-            out=out_1[0].rearrange("p m i -> p (m i)").bitcast(I32), in_=y_codes[:].bitcast(I32)
-        )
-        for q in range(4):
-            queue = nc.scalar if q % 2 == 0 else nc.sync
+        y_codes, y_scales = quantise(weave(y, WEAVE_SHARE), "y")
+        nc.sync.dma_start(out=out_1[0].rearrange("p m i -> p (m i)").bitcast(I32), in_=y_codes[:].bitcast(I32))
+        for quad in range(QUADS):
+            queue = nc.scalar if quad % 2 == 0 else nc.sync
             queue.dma_start(
-                out=out_2[0, 4 * q : 4 * q + 4, :].bitcast(I32), in_=y_scales[32 * q : 32 * q + 4, :].bitcast(I32)
+                out=out_2[0, 4 * quad : 4 * quad + 4, :].bitcast(I32),
+                in_=y_scales[32 * quad : 32 * quad + 4, :].bitcast(I32),
             )

@@ -30,6 +30,7 @@ PER_COLUMN = 16
 
 WEAVE_SHARE = 40
 FIRST_WEIGHT_SHARE = 64
+EARLY_MAXIMA = 2
 
 
 def tile_list_photochromic_fatigue_features_kernel(
@@ -39,7 +40,7 @@ def tile_list_photochromic_fatigue_features_kernel(
     nc = tc.nc
     with ExitStack() as ctx:
         keep = ctx.enter_context(tc.tile_pool(name="keep", bufs=1))
-        raw = ctx.enter_context(tc.tile_pool(name="raw", bufs=7))
+        raw = ctx.enter_context(tc.tile_pool(name="raw", bufs=6))
         rounded = ctx.enter_context(tc.tile_pool(name="rounded", bufs=4))
         psum = ctx.enter_context(tc.psum_pool(name="psum", bufs=1))
 
@@ -58,13 +59,14 @@ def tile_list_photochromic_fatigue_features_kernel(
             if scalar_share < P:
                 nc.vector.tensor_copy(out=dst[:, scalar_share:], in_=src[:, scalar_share:])
 
-        def load_weight(rows):
-            tile = raw.tile([P, PACK, GROUP], F32, name="raw")
+        def raw_tile():
+            return raw.tile([P, PACK, GROUP], F32, name="raw")
+
+        def load_weight(rows, tile):
             nc.sync.dma_start(out=tile[:], in_=rows.rearrange("(p i) c -> p i c", i=PACK))
             return tile
 
-        def deal(src, scalar_share):
-            dst = rounded_tile()
+        def deal(src, scalar_share, dst):
             shared_copy(
                 dst[:].rearrange("p (t q i) -> p q i t", t=PACK, i=PACK),
                 src[:].rearrange("p i (q t) -> p q i t", t=PACK),
@@ -108,7 +110,8 @@ def tile_list_photochromic_fatigue_features_kernel(
             )
 
         def load_w1(b, a):
-            w1_raw[b, a] = load_weight(w1[a * GROUP : (a + 1) * GROUP, b * GROUP : (b + 1) * GROUP])
+            tile = kept([P, PACK, GROUP], F32, "gate0") if (b, a) == (1, K_GROUPS - 2) else raw_tile()
+            w1_raw[b, a] = load_weight(w1[a * GROUP : (a + 1) * GROUP, b * GROUP : (b + 1) * GROUP], tile)
 
         def load_lamp(b, t):
             h[b, t] = kept([P, S], F32, "h%d%d" % (b, t))
@@ -146,21 +149,17 @@ def tile_list_photochromic_fatigue_features_kernel(
         load_w1(0, 2)
         pos1_sb = load_list(pos1, M, "pos1_sb")
         thr_sb = load_row_values(thr, "look_bias")
-        load_lamp(0, 0)
-        load_w1(1, 0)
-        load_lamp(0, 1)
-        load_w1(1, 1)
-        load_lamp(0, 2)
-        load_lamp(0, 3)
-        load_w1(1, 2)
+        for t in range(PACK):
+            load_lamp(0, t)
+            if t < K_GROUPS:
+                load_w1(1, t)
         tint_sb = load_row_values(tint, "tint_sb")
         pos2_sb = load_list(pos2, M, "pos2_sb")
-        w3_raw = {0: load_weight(w3[:GROUP, :])}
         for t in range(PACK):
             load_lamp(1, t)
         for b in range(H_GROUPS):
             load_wear(b)
-        w3_raw[1] = load_weight(w3[GROUP:, :])
+        w3_raw = [load_weight(w3[b * GROUP : (b + 1) * GROUP, :], raw_tile()) for b in range(H_GROUPS)]
 
         w2_dealt = kept([P, H_GROUPS, 2 * N], U8, "w2_dealt")
         nc.vector.tensor_copy(
@@ -202,7 +201,8 @@ def tile_list_photochromic_fatigue_features_kernel(
 
         acc = first_banks()
         for a in range(K_GROUPS):
-            weight = quantise(deal(w1_raw[0, a], FIRST_WEIGHT_SHARE if a == K_GROUPS - 1 else P), "w1_0%d" % a)
+            share = FIRST_WEIGHT_SHARE if a == K_GROUPS - 1 else P
+            weight = quantise(deal(w1_raw[0, a], share, rounded_tile()), "w1_0%d" % a)
             for half in range(S_BANKS):
                 picked[a, half] = kept([P, BANK], U32, "picked%d%d" % (a, half))
                 entries = offs_sb[:, half * BANK // PER_COLUMN : (half + 1) * BANK // PER_COLUMN]
@@ -215,7 +215,9 @@ def tile_list_photochromic_fatigue_features_kernel(
         for t in range(PACK):
             score(acc, 0, t)
         acc = first_banks()
-        weights = [quantise(deal(w1_raw[1, a], 0 if a == K_GROUPS - 1 else P), "w1_1%d" % a) for a in range(K_GROUPS)]
+        weights = [quantise(deal(w1_raw[1, a], P, rounded_tile()), "w1_1%d" % a) for a in range(K_GROUPS - 1)]
+        last_dealt = deal(w1_raw[1, K_GROUPS - 1], 0, kept([P, PACK * GROUP], BF16, "last_dealt"))
+        weights.append(quantise(last_dealt, "w1_last"))
         for t in range(PACK):
             first_product(acc, 0, weights[0], t)
         for t in range(PACK):
@@ -223,7 +225,6 @@ def tile_list_photochromic_fatigue_features_kernel(
                 first_product(acc, a, weights[a], t)
         for t in range(PACK):
             look_gate(0, t)
-        w3_dealt = {0: deal(w3_raw[0], P)}
         for t in range(PACK):
             score(acc, 1, t)
             look_gate(1, t)
@@ -234,12 +235,19 @@ def tile_list_photochromic_fatigue_features_kernel(
             in_=w2_scales_raw[:].rearrange("p b (q t) -> p b q t", t=PACK),
         )
 
-        top = keep.tile([P, H_GROUPS, PACK], F32, name="top")
         neg_top = keep.tile([P, H_GROUPS, PACK], F32, name="look_bias")
-        for b in range(H_GROUPS):
-            for t in range(PACK):
-                nc.vector.reduce_max(out=top[:, b, t : t + 1], in_=h[b, t][:], axis=AXIS.X)
-            nc.vector.tensor_scalar(out=neg_top[:, b, :], in0=top[:, b, :], scalar1=-1.0, scalar2=None, op0=ALU.mult)
+
+        def negated_maxima(b, slices, name):
+            top = kept([P, len(slices)], F32, name)
+            for j, t in enumerate(slices):
+                nc.vector.reduce_max(out=top[:, j : j + 1], in_=h[b, t][:], axis=AXIS.X)
+            nc.scalar.activation(
+                out=neg_top[:, b, slices.start : slices.stop], in_=top[:], func=ACT.Copy, scale=-1.0
+            )
+
+        negated_maxima(0, range(EARLY_MAXIMA), "top_early")
+        negated_maxima(0, range(EARLY_MAXIMA, PACK), "last_dealt")
+        negated_maxima(1, range(PACK), "top_last")
 
         worn_acc = [bank(t) for t in range(PACK)]
         joint_acc = [bank(PACK + t) for t in range(PACK)]
@@ -278,11 +286,12 @@ def tile_list_photochromic_fatigue_features_kernel(
                 lhs = w2_dealt[:, b, 2 * t * P : 2 * (t + 1) * P].bitcast(FP4X4)
                 second_product(joint_acc[t], b, lhs, w2_scales_dealt[:, b, t * P : (t + 1) * P], moving)
 
-        worn_product(0, worn_values(0, nc.vector))
+        w3_dealt = {0: deal(w3_raw[0], P, rounded_tile())}
+        worn_product(0, worn_values(0, nc.gpsimd))
         d_last = worn_values(1, nc.vector)
         joint_product(0, 0)
         joint_product(1, WEAVE_SHARE)
-        w3_dealt[1] = deal(w3_raw[1], P)
+        w3_dealt[1] = deal(w3_raw[1], P, rounded_tile())
         worn_product(1, d_last)
 
         y = kept([P, PACK, M], F32, "c0")

from contextlib import ExitStack

import concourse.mybir as mybir

K, T, S, H, M, N = 1536, 2048, 1024, 1024, 512, 512
FLOPS = 2 * K * H * S + 2 * 2 * H * N * M

F32 = mybir.dt.float32
BF16 = mybir.dt.bfloat16
I32 = mybir.dt.int32
U32 = mybir.dt.uint32
U16 = mybir.dt.uint16
U8 = mybir.dt.uint8
FP8X4 = mybir.dt.float8_e4m3fn_x4
FP4X4 = mybir.dt.float4_e2m1fn_x4
ACT = mybir.ActivationFunctionType
ALU = mybir.AluOpType
AXIS = mybir.AxisListType

P = 128
PACK = 4
GROUP = P * PACK
K_GROUPS = K // GROUP
H_GROUPS = H // GROUP
BANK = 512
S_BANKS = S // BANK
QUADS = 4
LINE = 4
PER_COLUMN = 16

WEAVE_SHARE = 40
FIRST_WEIGHT_SHARE = 64
EARLY_MAXIMA = 2


def tile_list_photochromic_fatigue_features_kernel(
    tc, tab_words, tab_scales, offs, pos1, pos2, w1, lamp, thr, tint, wear, w2_words, w2_scales, w3,
    out_0, out_1, out_2,
):
    nc = tc.nc
    with ExitStack() as ctx:
        keep = ctx.enter_context(tc.tile_pool(name="keep", bufs=1))
        raw = ctx.enter_context(tc.tile_pool(name="raw", bufs=6))
        rounded = ctx.enter_context(tc.tile_pool(name="rounded", bufs=4))
        psum = ctx.enter_context(tc.psum_pool(name="psum", bufs=1))

        def kept(shape, dtype, name):
            return keep.tile(shape, dtype, name=name, align_bytes=64)

        def bank(i):
            return psum.tile([P, BANK], F32, name="bank%d" % i)

        def rounded_tile():
            return rounded.tile([P, PACK * GROUP], BF16, name="rounded", align_bytes=64)

        def shared_copy(dst, src, scalar_share):
            if scalar_share > 0:
                nc.scalar.copy(out=dst[:, :scalar_share], in_=src[:, :scalar_share])
            if scalar_share < P:
                nc.vector.tensor_copy(out=dst[:, scalar_share:], in_=src[:, scalar_share:])

        def raw_tile():
            return raw.tile([P, PACK, GROUP], F32, name="raw")

        def load_weight(rows, tile):
            nc.sync.dma_start(out=tile[:], in_=rows.rearrange("(p i) c -> p i c", i=PACK))
            return tile

        def deal(src, scalar_share, dst):
            shared_copy(
                dst[:].rearrange("p (t q i) -> p q i t", t=PACK, i=PACK),
                src[:].rearrange("p i (q t) -> p q i t", t=PACK),
                scalar_share,
            )
            return dst

        def woven(tile):
            return tile[:].rearrange("p (c e t) -> p c t e", e=LINE, t=PACK)

        def by_lines(tile):
            return tile[:].rearrange("p t (c e) -> p c t e", e=LINE)

        def weave(src, scalar_share):
            dst = rounded_tile()
            shared_copy(woven(dst), by_lines(src), scalar_share)
            return dst

        def quantise(src, name):
            codes = kept([P, GROUP], U32, name + "_codes")
            scales = kept([P, GROUP], U8, name + "_scales")
            nc.vector.quantize_mx(out=codes[:].bitcast(FP8X4), scales=scales[:], in_=src[:])
            return codes, scales

        def load_list(src, entries, name):
            tile = keep.tile([P, entries // PER_COLUMN], U16, name=name)
            nc.sync.dma_start(tile[:], src)
            return tile

        def load_row_values(src, name):
            tile = keep.tile([P, H_GROUPS, PACK], F32, name=name)
            nc.sync.dma_start(out=tile[:], in_=src.rearrange("(b p t) -> p b t", p=P, t=PACK))
            return tile

        table, w1_raw, h, wear_sb = {}, {}, {}, {}

        def load_table(a):
            table[a] = kept([P, T], U32, "table%d" % a)
            nc.sync.dma_start(
                out=table[a][:].bitcast(I32), in_=tab_words[a].rearrange("p n i -> p (n i)").bitcast(I32)
            )

        def load_w1(b, a):
            tile = kept([P, PACK, GROUP], F32, "gate0") if (b, a) == (1, K_GROUPS - 2) else raw_tile()
            w1_raw[b, a] = load_weight(w1[a * GROUP : (a + 1) * GROUP, b * GROUP : (b + 1) * GROUP], tile)

        def load_lamp(b, t):
            h[b, t] = kept([P, S], F32, "h%d%d" % (b, t))
            rows = lamp[b * GROUP : (b + 1) * GROUP, :].rearrange("(p t) s -> p t s", t=PACK)
            nc.sync.dma_start(out=h[b, t][:], in_=rows[:, t, :])

        def load_wear(b):
            wear_sb[b] = kept([P, PACK, M], F32, "wear%d" % b)
            rows = wear[b * GROUP : (b + 1) * GROUP, :].rearrange("(p t) m -> p t m", t=PACK)
            nc.sync.dma_start(out=wear_sb[b][:], in_=rows)

        table_scales = kept([P, T], U8, "table_scales")
        nc.vector.memset(table_scales[:].bitcast(I32), 0)
        w2_scales_raw = kept([P, H_GROUPS, N], U8, "w2_scales_raw")
        nc.gpsimd.memset(w2_scales_raw[:].rearrange("p b n -> p (b n)").bitcast(I32), 0)

        offs_sb = load_list(offs, S, "offs_sb")
        w2_raw = kept([P, H_GROUPS, 2 * N], U8, "w2_raw")
        nc.sync.dma_start(out=w2_raw[:].bitcast(I32), in_=w2_words.rearrange("b p n -> p b n").bitcast(I32))
        load_table(0)
        load_w1(0, 0)
        for quad in range(QUADS):
            nc.sync.dma_start(
                out=table_scales[32 * quad : 32 * quad + 4 * K_GROUPS, :].bitcast(I32),
                in_=tab_scales[:, 4 * quad : 4 * quad + 4, :].bitcast(I32),
            )
        load_table(1)
        load_w1(0, 1)
        for quad in range(QUADS):
            nc.sync.dma_start(
                out=w2_scales_raw[32 * quad : 32 * quad + 4].bitcast(I32),
                in_=w2_scales[:, 4 * quad : 4 * quad + 4, :].rearrange("b r n -> r b n").bitcast(I32),
            )
        load_table(2)
        load_w1(0, 2)
        pos1_sb = load_list(pos1, M, "pos1_sb")
        thr_sb = load_row_values(thr, "look_bias")
        for t in range(PACK):
            load_lamp(0, t)
            if t < K_GROUPS:
                load_w1(1, t)
        tint_sb = load_row_values(tint, "tint_sb")
        pos2_sb = load_list(pos2, M, "pos2_sb")
        for t in range(PACK):
            load_lamp(1, t)
        for b in range(H_GROUPS):
            load_wear(b)
        w3_raw = [load_weight(w3[b * GROUP : (b + 1) * GROUP, :], raw_tile()) for b in range(H_GROUPS)]

        w2_dealt = kept([P, H_GROUPS, 2 * N], U8, "w2_dealt")
        nc.vector.tensor_copy(
            out=w2_dealt[:].rearrange("p b (t q e) -> p b q t e", t=PACK, e=2),
            in_=w2_raw[:].rearrange("p b (q t e) -> p b q t e", t=PACK, e=2),
        )

        picked = {}
        picked_scales = kept([P, S], U8, "picked_scales")

        def first_product(acc, a, weight, t):
            codes, scales = weight
            for half in range(S_BANKS):
                nc.tensor.matmul_mx(
                    out=acc[t, half][:],
                    lhsT=codes[:, t * P : (t + 1) * P].bitcast(FP8X4),
                    lhsT_scale=scales[:, t * P : (t + 1) * P],
                    rhs=picked[a, half][:].bitcast(FP8X4),
                    rhs_scale=picked_scales[4 * a : P, half * BANK : (half + 1) * BANK],
                    start=(a == 0),
                    stop=(a == K_GROUPS - 1),
                )

        def first_banks():
            return {(t, half): bank(S_BANKS * t + half) for t in range(PACK) for half in range(S_BANKS)}

        def score(acc, b, t):
            for half in range(S_BANKS):
                part = h[b, t][:, half * BANK : (half + 1) * BANK]
                nc.vector.tensor_tensor(out=part, in0=acc[t, half][:], in1=part, op=ALU.mult)

        gate = {b: kept([P, PACK, M], F32, "gate%d" % b) for b in range(H_GROUPS)}

        def look_gate(b, t):
            nc.scalar.activation(
                out=gate[b][:, t, :], in_=h[b, t][:].indirect(pos1_sb[:]), func=ACT.Sigmoid,
                bias=thr_sb[:, b, t : t + 1],
            )

        acc = first_banks()
        for a in range(K_GROUPS):
            share = FIRST_WEIGHT_SHARE if a == K_GROUPS - 1 else P
            weight = quantise(deal(w1_raw[0, a], share, rounded_tile()), "w1_0%d" % a)
            for half in range(S_BANKS):
                picked[a, half] = kept([P, BANK], U32, "picked%d%d" % (a, half))
                entries = offs_sb[:, half * BANK // PER_COLUMN : (half + 1) * BANK // PER_COLUMN]
                nc.vector.tensor_copy(out=picked[a, half][:], in_=table[a][:].indirect(entries))
            if a == 0:
                nc.vector.tensor_copy(out=picked_scales[:], in_=table_scales[:].indirect(offs_sb[:]))
            for t in range(PACK):
                first_product(acc, a, weight, t)

        for t in range(PACK):
            score(acc, 0, t)
        acc = first_banks()
        weights = [quantise(deal(w1_raw[1, a], P, rounded_tile()), "w1_1%d" % a) for a in range(K_GROUPS - 1)]
        last_dealt = deal(w1_raw[1, K_GROUPS - 1], 0, kept([P, PACK * GROUP], BF16, "last_dealt"))
        weights.append(quantise(last_dealt, "w1_last"))
        for t in range(PACK):
            first_product(acc, 0, weights[0], t)
        for t in range(PACK):
            for a in range(1, K_GROUPS):
                first_product(acc, a, weights[a], t)
        for t in range(PACK):
            look_gate(0, t)
        for t in range(PACK):
            score(acc, 1, t)
            look_gate(1, t)

        w2_scales_dealt = kept([P, H_GROUPS, N], U8, "w2_scales_dealt")
        nc.vector.tensor_copy(
            out=w2_scales_dealt[:].rearrange("p b (t q) -> p b q t", t=PACK),
            in_=w2_scales_raw[:].rearrange("p b (q t) -> p b q t", t=PACK),
        )

        neg_top = keep.tile([P, H_GROUPS, PACK], F32, name="look_bias")

        def negated_maxima(b, slices, name):
            top = kept([P, len(slices)], F32, name)
            for j, t in enumerate(slices):
                nc.vector.reduce_max(out=top[:, j : j + 1], in_=h[b, t][:], axis=AXIS.X)
            nc.scalar.activation(
                out=neg_top[:, b, slices.start : slices.stop], in_=top[:], func=ACT.Copy, scale=-1.0
            )

        negated_maxima(0, range(EARLY_MAXIMA), "top_early")
        negated_maxima(0, range(EARLY_MAXIMA, PACK), "last_dealt")
        negated_maxima(1, range(PACK), "top_last")

        worn_acc = [bank(t) for t in range(PACK)]
        joint_acc = [bank(PACK + t) for t in range(PACK)]

        def second_product(out, b, lhs, lhs_scale, moving):
            codes, scales = moving
            nc.tensor.matmul_mx(
                out=out[:], lhsT=lhs, lhsT_scale=lhs_scale, rhs=codes[:].bitcast(FP8X4), rhs_scale=scales[:],
                start=(b == 0), stop=(b == H_GROUPS - 1),
            )

        def worn_values(b, engine):
            d = rounded_tile()
            engine.tensor_tensor(out=woven(d), in0=by_lines(gate[b]), in1=by_lines(wear_sb[b]), op=ALU.mult)
            return d

        def worn_product(b, d):
            moving = quantise(d, "d%d" % b)
            codes, scales = quantise(w3_dealt[b], "w3_%d" % b)
            for t in range(PACK):
                cols = slice(t * P, (t + 1) * P)
                second_product(worn_acc[t], b, codes[:, cols].bitcast(FP8X4), scales[:, cols], moving)

        def joint_product(b, scalar_share):
            c = kept([P, PACK, M], F32, "c%d" % b)
            for t in range(PACK):
                nc.scalar.activation(
                    out=c[:, t, :], in_=h[b, t][:].indirect(pos2_sb[:]), func=ACT.Exp, bias=neg_top[:, b, t : t + 1]
                )
                nc.vector.scalar_tensor_tensor(
                    out=c[:, t, :], in0=gate[b][:, t, :], scalar=tint_sb[:, b, t : t + 1], in1=c[:, t, :],
                    op0=ALU.mult, op1=ALU.mult,
                )
            moving = quantise(weave(c, scalar_share), "f%d" % b)
            for t in range(PACK):
                lhs = w2_dealt[:, b, 2 * t * P : 2 * (t + 1) * P].bitcast(FP4X4)
                second_product(joint_acc[t], b, lhs, w2_scales_dealt[:, b, t * P : (t + 1) * P], moving)

        w3_dealt = {0: deal(w3_raw[0], P, rounded_tile())}
        worn_product(0, worn_values(0, nc.gpsimd))
        d_last = worn_values(1, nc.vector)
        joint_product(0, 0)
        joint_product(1, WEAVE_SHARE)
        w3_dealt[1] = deal(w3_raw[1], P, rounded_tile())
        worn_product(1, d_last)

        y = kept([P, PACK, M], F32, "c0")
        y_rows = out_0.rearrange("(p t) m -> p t m", t=PACK)
        for t in range(PACK):
            nc.scalar.copy(out=y[:, t, :], in_=worn_acc[t][:])
        for t in range(PACK):
            nc.vector.tensor_tensor(out=y[:, t, :], in0=joint_acc[t][:], in1=y[:, t, :], op=ALU.min)
            nc.sync.dma_start(out=y_rows[:, t, :], in_=y[:, t, :])
        y_codes, y_scales = quantise(weave(y, WEAVE_SHARE), "y")
        nc.sync.dma_start(out=out_1[0].rearrange("p m i -> p (m i)").bitcast(I32), in_=y_codes[:].bitcast(I32))
        for quad in range(QUADS):
            queue = nc.scalar if quad % 2 == 0 else nc.sync
            queue.dma_start(
                out=out_2[0, 4 * quad : 4 * quad + 4, :].bitcast(I32),
                in_=y_scales[32 * quad : 32 * quad + 4, :].bitcast(I32),
            )
